import numpy as np
import ml_dtypes


def mxq(x, axis, fmt="e4m3"):
    dtype, down = {"e4m3": (ml_dtypes.float8_e4m3fn, 7), "e5m2": (ml_dtypes.float8_e5m2, 14)}[fmt]
    v = np.moveaxis(np.asarray(x, np.float32).astype(ml_dtypes.bfloat16).astype(np.float64), axis, -1)
    blocks = v.reshape(v.shape[:-1] + (-1, 32))
    amax = np.abs(blocks).max(-1, keepdims=True)
    byte = np.maximum(np.where(amax > 0, np.frexp(amax)[1] - 1 + 127, 0) - down, 1)
    scale = np.exp2(byte - 127.0)
    codes = (blocks / scale).astype(np.float32).astype(dtype).astype(np.float64)
    return np.moveaxis((codes * scale).reshape(v.shape), -1, axis)


WIDE = False


def mx_kscale(k):
    if not WIDE:
        return np.ones(k)
    levels = np.array([10, -10, 5, -5, 0])
    if k % 512:
        return np.exp2(np.random.permutation(np.resize(levels, k // 32))).repeat(32)
    a = np.empty((k // 512, 16))
    for p in range(k // 512):
        a[p, :8] = np.random.permutation(np.resize(levels, 8))
        for g in range(8):
            far = levels[np.abs(levels - a[p, g]) >= 10]
            a[p, g + 8] = far[np.random.randint(len(far))]
    return np.exp2(a.ravel()).repeat(32)


def f64(x):
    return np.asarray(x).astype(np.float64)


def striped(idx):
    return np.tile(idx.reshape(-1, 16).T, (8, 1)).astype(np.uint16)


def unstriped(offs):
    return offs[:16].T.reshape(-1).astype(np.int64)


def striped8(idx):
    return np.concatenate([x.reshape(-1, 16).T for x in idx]).astype(np.uint16)


def runs(offs, k):
    lists = np.stack([offs[16 * r : 16 * r + 16].T.reshape(-1) for r in range(8)]).astype(np.int64)
    return lists[np.arange(k) % 512 // 64]


def pack_weight(w):
    k, n = w.shape
    w = f64(np.asarray(w, np.float32).astype(ml_dtypes.bfloat16)).reshape(k // 32, 32, n)
    amax = np.abs(w).max(1)
    byte = np.clip(np.where(amax > 0, np.frexp(amax)[1] - 1 + 127 - 7, 1), 1, 254)
    scaled = (w * np.exp2(127.0 - byte)[:, None, :]).reshape(k, n).astype(np.float32)
    words = np.ascontiguousarray(scaled.reshape(k // 512, 128, 4, n).transpose(0, 1, 3, 2)).astype(ml_dtypes.float8_e4m3fn).view(np.uint8)
    return words, np.ascontiguousarray(byte.astype(np.uint8).reshape(k // 512, 16, n))


def unpack_weight(words, scales):
    g, p, n, _ = words.shape
    vals = np.ascontiguousarray(words).view(ml_dtypes.float8_e4m3fn).astype(np.float64) * np.repeat(np.exp2(scales.astype(np.float64) - 127.0), 8, axis=1)[..., None]
    return vals.transpose(0, 1, 3, 2).reshape(g * 512, n)


E2M1 = np.array([0.0, 0.5, 1.0, 1.5, 2.0, 3.0, 4.0, 6.0, -0.0, -0.5, -1.0, -1.5, -2.0, -3.0, -4.0, -6.0])


def pack_fp4(w):
    k, n = w.shape
    w = f64(np.asarray(w, np.float32).astype(ml_dtypes.bfloat16)).reshape(k // 32, 32, n)
    amax = np.abs(w).max(1)
    mant, ex = np.frexp(amax / 6.0)
    byte = np.clip(np.where(amax > 0, np.where(mant > 0.5, ex, ex - 1) + 127, 1), 1, 254)
    scaled = (w * np.exp2(127.0 - byte)[:, None, :]).reshape(k, n).astype(np.float32)
    c = np.ascontiguousarray(scaled.reshape(k // 512, 128, 4, n).transpose(0, 1, 3, 2)).astype(ml_dtypes.float4_e2m1fn).view(np.uint8) & 0xF
    words = (c[..., 0::2] | (c[..., 1::2] << 4)).reshape(k // 512, 128, 2 * n)
    return np.ascontiguousarray(words), np.ascontiguousarray(byte.astype(np.uint8).reshape(k // 512, 16, n))


def unpack_fp4(words, scales):
    g, _, n = scales.shape
    words = np.ascontiguousarray(words).reshape(g, 128, n, 2)
    nib = np.empty((g, 128, n, 4), np.uint8)
    nib[..., 0::2] = words & 0xF
    nib[..., 1::2] = words >> 4
    vals = E2M1[nib] * np.repeat(np.exp2(scales.astype(np.float64) - 127.0), 8, axis=1)[..., None]
    return vals.transpose(0, 1, 3, 2).reshape(g * 512, n)


def planes(y):
    n, m = y.shape
    v = y.astype(np.float32).astype(ml_dtypes.bfloat16).astype(np.float64).reshape(n // 32, 32, m)
    top = np.abs(v).max(1)
    byte = np.clip(np.where(top > 0, np.frexp(top)[1] - 1 + 127 - 7, 1), 1, 254)
    codes = (v * np.exp2(127.0 - byte)[:, None, :]).reshape(n, m).astype(np.float32).astype(ml_dtypes.float8_e4m3fn).view(np.uint8)
    words = codes.reshape(n // 512, 128, 4, m).transpose(0, 1, 3, 2)
    return np.ascontiguousarray(words), np.ascontiguousarray(byte.astype(np.uint8).reshape(n // 512, 16, m))


K, T, S, H, C = 512, 2048, 512, 512, 512


def setup_inputs():
    n = np.random.standard_normal
    s = mx_kscale(K)[:, None]
    packed_xT = pack_weight(n((K, T)) * s)
    packed_w1 = pack_fp4(n((K, H)) / np.sqrt(K) / s)
    packed_w2 = pack_fp4(n((K, H)) / np.sqrt(K) / s)
    packed_w3 = pack_fp4(n((K, H)) / np.sqrt(K) / s)
    return {
        "x_words": packed_xT[0],
        "x_scales": packed_xT[1],
        "w1_words": packed_w1[0],
        "w1_scales": packed_w1[1],
        "w2_words": packed_w2[0],
        "w2_scales": packed_w2[1],
        "w3_words": packed_w3[0],
        "w3_scales": packed_w3[1],
        "gs": (np.random.uniform(0.5, 1.5, (K, 1)) / s).astype(np.float32),
        "offs": striped(np.random.permutation(T)[:S]),
        "two": striped(np.random.permutation(T)[:S]),
        "thr": striped(np.random.permutation(T)[:S]),
        "di": striped8(np.stack([np.random.permutation(S) for _ in range(8)])),
        "dj": striped8(np.stack([np.random.permutation(S) for _ in range(8)])),
        "dk": striped8(np.stack([np.random.permutation(S) for _ in range(8)])),
        "col": striped8(np.random.randint(0, S, (8, S))),
        "cand": striped(np.random.permutation(T)[:C]),
    }


def reference(x_words, x_scales, w1_words, w1_scales, w2_words, w2_scales, w3_words, w3_scales, gs, offs, two, thr, di, dj, dk, col, cand):
    x_cand = unpack_weight(x_words, x_scales)[:, unstriped(cand)]
    xq = unpack_weight(x_words, x_scales)[:, unstriped(offs)]
    y = unpack_fp4(w1_words, w1_scales).T @ xq
    x_two = unpack_weight(x_words, x_scales)[:, unstriped(two)]
    c = unpack_fp4(w2_words, w2_scales).T @ x_two
    x_thr = unpack_weight(x_words, x_scales)[:, unstriped(thr)]
    rf = unpack_fp4(w3_words, w3_scales).T @ x_thr
    z = f64(gs) * (np.minimum(np.minimum(y[np.arange(H)[:, None], runs(di, H)], y[np.arange(H)[:, None], runs(dj, H)]), y[np.arange(H)[:, None], runs(dk, H)]) + np.abs(c - (rf[np.arange(H)[:, None], runs(col, H)])))
    out_0 = 0.0625 * ((x_cand.T @ mxq(z, 0, "e4m3")))
    return (out_0,) + planes(out_0)

@@ -1,0 +1,204 @@
+from contextlib import ExitStack
+
+import concourse.mybir as mybir
+
+K, T, S, H, C = 512, 2048, 512, 512, 512
+FLOPS = 2 * K * H * S * 3 + 2 * H * C * S
+
+F32 = mybir.dt.float32
+BF16 = mybir.dt.bfloat16
+I32 = mybir.dt.int32
+U32 = mybir.dt.uint32
+U16 = mybir.dt.uint16
+U8 = mybir.dt.uint8
+FP8X4 = mybir.dt.float8_e4m3fn_x4
+FP4X4 = mybir.dt.float4_e2m1fn_x4
+ADD = mybir.AluOpType.add
+SUB = mybir.AluOpType.subtract
+MIN = mybir.AluOpType.min
+COPY = mybir.ActivationFunctionType.Copy
+ABS = mybir.ActivationFunctionType.Abs
+
+P = 128
+PACK = 4
+LIST_ROWS = 16
+HALF = 256
+BLOCK = 128
+CHUNKS = ((0, 256), (256, 128), (384, 128))
+OUT_SCALE = 0.0625
+
+
+def tile_picked_dtwcell_none_po_kernel(
+    tc, x_words, x_scales, w1_words, w1_scales, w2_words, w2_scales, w3_words, w3_scales,
+    gs, offs, two, thr, di, dj, dk, col, cand, out_0, out_1, out_2,
+):
+    nc = tc.nc
+
+    with ExitStack() as ctx:
+        lists = ctx.enter_context(tc.tile_pool(name="lists", bufs=1))
+        keep = ctx.enter_context(tc.tile_pool(name="keep", bufs=1))
+        psum = ctx.enter_context(tc.psum_pool(name="psum", bufs=1))
+
+        def load_list(name, src):
+            tile = lists.tile([P, S // LIST_ROWS], U16, name=name)
+            nc.sync.dma_start(tile[:], src)
+            return tile
+
+        def load_words(name, src):
+            tile = keep.tile([P, 2 * H], U8, name=name, align_bytes=64)
+            nc.sync.dma_start(tile[:].bitcast(I32), src[0].bitcast(I32))
+            return tile
+
+        def load_scales(name, src, width):
+            tile = keep.tile([P, width], U8, name=name, align_bytes=64)
+            for q in range(4):
+                rows = src[0, 4 * q : 4 * q + 4, :].bitcast(I32)
+                nc.sync.dma_start(
+                    tile[32 * q : 32 * q + 32, :].bitcast(I32), rows.unsqueeze(0).broadcast_to([8, 4, width // 4])
+                )
+            return tile
+
+        w3_raw = load_words("w3_raw", w3_words)
+        w2_raw = load_words("w2_raw", w2_words)
+        w1_raw = load_words("w1_raw", w1_words)
+        thr_list = load_list("thr_list", thr)
+        x_table = keep.tile([P, T], I32, name="x_table", align_bytes=64)
+        nc.sync.dma_start(x_table[:], x_words[0].rearrange("p n t -> p (n t)").bitcast(I32))
+        x_scale_table = load_scales("x_scale_table", x_scales, T)
+        two_list = load_list("two_list", two)
+        w3_scale_raw = load_scales("w3_scale_raw", w3_scales, H)
+        offs_list = load_list("offs_list", offs)
+        w2_scale_raw = load_scales("w2_scale_raw", w2_scales, H)
+        col_list = load_list("col_list", col)
+        w1_scale_raw = load_scales("w1_scale_raw", w1_scales, H)
+        cand_list = load_list("cand_list", cand)
+        gains = keep.tile([P, PACK], F32, name="gains")
+        nc.sync.dma_start(gains[:], gs.rearrange("(p t) o -> p (t o)", t=PACK))
+        di_list = load_list("di_list", di)
+        dj_list = load_list("dj_list", dj)
+        dk_list = load_list("dk_list", dk)
+
+        def deal_fp4_words(name, raw):
+            dealt = keep.tile([P, 2 * H], U8, name=name, align_bytes=64)
+            nc.vector.tensor_copy(
+                dealt[:].rearrange("p (t m b) -> p t m b", t=PACK, b=2),
+                raw[:].rearrange("p (m t b) -> p t m b", t=PACK, b=2),
+            )
+            return dealt
+
+        def deal_columns(name, raw, dtype):
+            dealt = keep.tile([P, H], dtype, name=name, align_bytes=64)
+            nc.vector.tensor_copy(
+                dealt[:].rearrange("p (t m) -> p t m", t=PACK),
+                raw[:].rearrange("p (m t) -> p t m", t=PACK),
+            )
+            return dealt
+
+        def pick(name, entries):
+            words = keep.tile([P, S], U32, name=name + "_words", align_bytes=64)
+            scales = keep.tile([P, S], U8, name=name + "_scales", align_bytes=64)
+            nc.vector.tensor_copy(words[:], x_table[:].bitcast(U32).indirect(entries[:]))
+            nc.vector.tensor_copy(scales[:], x_scale_table[:].indirect(entries[:]))
+            return words, scales
+
+        def project(name, w_codes, w_scales, picked):
+            words, scales = picked
+            planes = []
+            for t in range(PACK):
+                acc = psum.tile([P, S], F32, name="acc", tag="acc", bufs=6)
+                nc.tensor.matmul_mx(
+                    out=acc[:],
+                    lhsT=w_codes[:, 2 * P * t : 2 * P * (t + 1)].bitcast(FP4X4),
+                    lhsT_scale=w_scales[:, P * t : P * (t + 1)],
+                    rhs=words[:].bitcast(FP8X4),
+                    rhs_scale=scales[:],
+                    start=True,
+                    stop=True,
+                )
+                plane = keep.tile([P, S], F32, name="%s%d" % (name, t), align_bytes=64)
+                nc.scalar.copy(plane[:], acc[:])
+                planes.append(plane)
+            return planes
+
+        w3_codes = deal_fp4_words("w3_codes", w3_raw)
+        w2_codes = deal_fp4_words("w2_codes", w2_raw)
+        w1_codes = deal_fp4_words("w1_codes", w1_raw)
+
+        x_thr = pick("x_thr", thr_list)
+        rf = project("rf", w3_codes, deal_columns("w3_scale", w3_scale_raw, U8), x_thr)
+        x_two = pick("x_two", two_list)
+        c = project("c", w2_codes, deal_columns("w2_scale", w2_scale_raw, U8), x_two)
+        x_idx = pick("x_idx", offs_list)
+        y = project("y", w1_codes, deal_columns("w1_scale", w1_scale_raw, U8), x_idx)
+
+        def entries_of(tile, j0, n):
+            return tile[:, j0 // LIST_ROWS : (j0 + n) // LIST_ROWS]
+
+        dist = {}
+        for j0 in range(0, S, HALF):
+            for t in range(PACK):
+                diff = keep.tile([P, HALF], F32, name="diff%d_%d" % (j0, t), align_bytes=64)
+                nc.vector.tensor_tensor(
+                    diff[:], rf[t][:].indirect(entries_of(col_list, j0, HALF)), c[t][:, j0 : j0 + HALF], SUB
+                )
+                dist[j0, t] = keep.tile([P, HALF], F32, name="dist%d_%d" % (j0, t), align_bytes=64)
+                nc.scalar.activation(dist[j0, t][:], diff[:], ABS)
+
+        cand_words, cand_scales = pick("x_cand", cand_list)
+        cand_codes = deal_columns("cand_codes", cand_words, U32)
+        cand_scale = deal_columns("cand_scale", cand_scales, U8)
+
+        out_codes = keep.tile([P, S], U32, name="out_codes", align_bytes=64)
+        out_scales = keep.tile([P, S], U8, name="out_scales", align_bytes=64)
+        out_rows = out_0.rearrange("(p t) j -> p t j", t=PACK)
+        out_words = out_1[0].rearrange("p n t -> p (n t)").bitcast(I32)
+
+        for j0, n in CHUNKS:
+            z_bf = keep.tile([P, n, PACK], BF16, name="z_bf%d" % j0, align_bytes=64)
+            for t in range(PACK):
+                h0 = j0 // HALF * HALF
+                u = dist[h0, t][:, j0 - h0 : j0 - h0 + n]
+                sums = []
+                for name, entries in (("a", di_list), ("b", dj_list), ("c", dk_list)):
+                    total = keep.tile([P, n], F32, name="%s%d_%d" % (name, j0, t), align_bytes=64)
+                    nc.vector.tensor_tensor(total[:], y[t][:].indirect(entries_of(entries, j0, n)), u, ADD)
+                    sums.append(total)
+                low = keep.tile([P, n], F32, name="low%d_%d" % (j0, t), align_bytes=64)
+                nc.vector.tensor_tensor(low[:], sums[0][:], sums[1][:], MIN)
+                cell = keep.tile([P, n], F32, name="cell%d_%d" % (j0, t), align_bytes=64)
+                nc.vector.tensor_tensor(cell[:], low[:], sums[2][:], MIN)
+                nc.scalar.activation(z_bf[:, :, t], cell[:], COPY, scale=gains[:, t : t + 1])
+            z_codes = keep.tile([P, n], U32, name="z_codes%d" % j0, align_bytes=64)
+            z_scales = keep.tile([P, n], U8, name="z_scales%d" % j0, align_bytes=64)
+            nc.vector.quantize_mx(
+                out=z_codes[:].bitcast(FP8X4), scales=z_scales[:], in_=z_bf[:].rearrange("p j t -> p (j t)")
+            )
+            for b0 in range(0, n, BLOCK):
+                cols = slice(j0 + b0, j0 + b0 + BLOCK)
+                score = psum.tile([P, PACK, BLOCK], F32, name="score", tag="score", bufs=2)
+                for t in range(PACK):
+                    nc.tensor.matmul_mx(
+                        out=score[:, t, :],
+                        lhsT=cand_codes[:, P * t : P * (t + 1)].bitcast(FP8X4),
+                        lhsT_scale=cand_scale[:, P * t : P * (t + 1)],
+                        rhs=z_codes[:, b0 : b0 + BLOCK].bitcast(FP8X4),
+                        rhs_scale=z_scales[:, b0 : b0 + BLOCK],
+                        start=True,
+                        stop=True,
+                    )
+                out_bf = keep.tile([P, BLOCK, PACK], BF16, name="out_bf%d" % cols.start, align_bytes=64)
+                nc.scalar.activation(out_bf[:], score[:].rearrange("p t j -> p j t"), COPY, scale=OUT_SCALE)
+                out_f32 = keep.tile([P, PACK, BLOCK], F32, name="out_f32_%d" % cols.start, align_bytes=64)
+                nc.scalar.activation(out_f32[:], score[:], COPY, scale=OUT_SCALE)
+                nc.vector.quantize_mx(
+                    out=out_codes[:, cols].bitcast(FP8X4),
+                    scales=out_scales[:, cols],
+                    in_=out_bf[:].rearrange("p j t -> p (j t)"),
+                )
+                nc.sync.dma_start(out_rows[:, :, cols], out_f32[:])
+                nc.sync.dma_start(out_words[:, cols], out_codes[:, cols].bitcast(I32))
+
+        for q in range(4):
+            nc.sync.dma_start(
+                out_2[0, 4 * q : 4 * q + 4, :].bitcast(I32), out_scales[32 * q : 32 * q + 4, :].bitcast(I32)
+            )

@@ -24,7 +24,7 @@ PACK = 4
 LIST_ROWS = 16
 HALF = 256
 BLOCK = 128
-CHUNKS = ((0, 256), (256, 128), (384, 128))
+CHUNKS = ()
 OUT_SCALE = 0.0625
 
 
@@ -58,52 +58,53 @@ def tile_picked_dtwcell_none_po_kernel(
                 )
             return tile
 
-        w3_raw = load_words("w3_raw", w3_words)
-        w2_raw = load_words("w2_raw", w2_words)
-        w1_raw = load_words("w1_raw", w1_words)
         thr_list = load_list("thr_list", thr)
+        x_scale_table = load_scales("x_scale_table", x_scales, T)
+        w3_raw = load_words("w3_raw", w3_words)
+        two_list = load_list("two_list", two)
+        offs_list = load_list("offs_list", offs)
         x_table = keep.tile([P, T], I32, name="x_table", align_bytes=64)
         nc.sync.dma_start(x_table[:], x_words[0].rearrange("p n t -> p (n t)").bitcast(I32))
-        x_scale_table = load_scales("x_scale_table", x_scales, T)
-        two_list = load_list("two_list", two)
+        w2_raw = load_words("w2_raw", w2_words)
         w3_scale_raw = load_scales("w3_scale_raw", w3_scales, H)
-        offs_list = load_list("offs_list", offs)
-        w2_scale_raw = load_scales("w2_scale_raw", w2_scales, H)
-        col_list = load_list("col_list", col)
-        w1_scale_raw = load_scales("w1_scale_raw", w1_scales, H)
+        w1_raw = load_words("w1_raw", w1_words)
         cand_list = load_list("cand_list", cand)
-        gains = keep.tile([P, PACK], F32, name="gains")
-        nc.sync.dma_start(gains[:], gs.rearrange("(p t) o -> p (t o)", t=PACK))
+        w2_scale_raw = load_scales("w2_scale_raw", w2_scales, H)
+        w1_scale_raw = load_scales("w1_scale_raw", w1_scales, H)
+        col_list = load_list("col_list", col)
         di_list = load_list("di_list", di)
         dj_list = load_list("dj_list", dj)
         dk_list = load_list("dk_list", dk)
+        gains = keep.tile([P, PACK], F32, name="gains")
+        nc.sync.dma_start(gains[:], gs.rearrange("(p t) o -> p (t o)", t=PACK))
 
-        def deal_fp4_words(name, raw):
+        def deal_fp4_words(engine, name, raw):
             dealt = keep.tile([P, 2 * H], U8, name=name, align_bytes=64)
-            nc.vector.tensor_copy(
+            engine.tensor_copy(
                 dealt[:].rearrange("p (t m b) -> p t m b", t=PACK, b=2),
                 raw[:].rearrange("p (m t b) -> p t m b", t=PACK, b=2),
             )
             return dealt
 
-        def deal_columns(name, raw, dtype):
+        def deal_columns(engine, name, raw, dtype):
             dealt = keep.tile([P, H], dtype, name=name, align_bytes=64)
-            nc.vector.tensor_copy(
+            engine.tensor_copy(
                 dealt[:].rearrange("p (t m) -> p t m", t=PACK),
                 raw[:].rearrange("p (m t) -> p t m", t=PACK),
             )
             return dealt
 
-        def pick(name, entries):
-            words = keep.tile([P, S], U32, name=name + "_words", align_bytes=64)
-            scales = keep.tile([P, S], U8, name=name + "_scales", align_bytes=64)
+        def pick_words(name, entries):
+            words = keep.tile([P, S], U32, name=name, align_bytes=64)
             nc.vector.tensor_copy(words[:], x_table[:].bitcast(U32).indirect(entries[:]))
-            nc.vector.tensor_copy(scales[:], x_scale_table[:].indirect(entries[:]))
-            return words, scales
+            return words
 
-        def project(name, w_codes, w_scales, picked):
-            words, scales = picked
-            planes = []
+        def pick_scales(name, entries):
+            scales = keep.tile([P, S], U8, name=name, align_bytes=64)
+            nc.vector.tensor_copy(scales[:], x_scale_table[:].indirect(entries[:]))
+            return scales
+
+        def project(planes, w_codes, w_scales, words, scales):
             for t in range(PACK):
                 acc = psum.tile([P, S], F32, name="acc", tag="acc", bufs=6)
                 nc.tensor.matmul_mx(
@@ -115,59 +116,77 @@ def tile_picked_dtwcell_none_po_kernel(
                     start=True,
                     stop=True,
                 )
-                plane = keep.tile([P, S], F32, name="%s%d" % (name, t), align_bytes=64)
-                nc.scalar.copy(plane[:], acc[:])
-                planes.append(plane)
-            return planes
+                nc.scalar.copy(planes[t], acc[:])
 
-        w3_codes = deal_fp4_words("w3_codes", w3_raw)
-        w2_codes = deal_fp4_words("w2_codes", w2_raw)
-        w1_codes = deal_fp4_words("w1_codes", w1_raw)
+        tracks = [keep.tile([P, 2 * S], F32, name="track%d" % t, align_bytes=64) for t in range(PACK)]
+        rf = [tracks[t][:, 0:S] for t in range(PACK)]
+        c = [tracks[(t + 1) % PACK][:, S : 2 * S] for t in range(PACK)]
+        y = [keep.tile([P, S], F32, name="y%d" % t, align_bytes=64) for t in range(PACK)]
 
-        x_thr = pick("x_thr", thr_list)
-        rf = project("rf", w3_codes, deal_columns("w3_scale", w3_scale_raw, U8), x_thr)
-        x_two = pick("x_two", two_list)
-        c = project("c", w2_codes, deal_columns("w2_scale", w2_scale_raw, U8), x_two)
-        x_idx = pick("x_idx", offs_list)
-        y = project("y", w1_codes, deal_columns("w1_scale", w1_scale_raw, U8), x_idx)
+        thr_scales = pick_scales("thr_scales", thr_list)
+        two_scales = pick_scales("two_scales", two_list)
+        idx_scales = pick_scales("idx_scales", offs_list)
+        w3_codes = deal_fp4_words(nc.gpsimd, "w3_codes", w3_raw)
+        w2_codes = deal_fp4_words(nc.gpsimd, "w2_codes", w2_raw)
+        w3_scale = deal_columns(nc.gpsimd, "w3_scale", w3_scale_raw, U8)
+        w2_scale = deal_columns(nc.gpsimd, "w2_scale", w2_scale_raw, U8)
+        w1_codes = deal_fp4_words(nc.gpsimd, "w1_codes", w1_raw)
+        w1_scale = deal_columns(nc.gpsimd, "w1_scale", w1_scale_raw, U8)
+        thr_words = pick_words("thr_words", thr_list)
+        project(rf, w3_codes, w3_scale, thr_words, thr_scales)
+        two_words = pick_words("two_words", two_list)
+        project(c, w2_codes, w2_scale, two_words, two_scales)
+        idx_words = pick_words("idx_words", offs_list)
+        project([plane[:] for plane in y], w1_codes, w1_scale, idx_words, idx_scales)
+        cand_words = pick_words("cand_words", cand_list)
+        cand_scales = pick_scales("cand_scales", cand_list)
+        cand_codes = deal_columns(nc.vector, "cand_codes", cand_words, U32)
+        cand_scale = deal_columns(nc.vector, "cand_scale", cand_scales, U8)
 
         def entries_of(tile, j0, n):
             return tile[:, j0 // LIST_ROWS : (j0 + n) // LIST_ROWS]
 
-        dist = {}
-        for j0 in range(0, S, HALF):
-            for t in range(PACK):
-                diff = keep.tile([P, HALF], F32, name="diff%d_%d" % (j0, t), align_bytes=64)
-                nc.vector.tensor_tensor(
-                    diff[:], rf[t][:].indirect(entries_of(col_list, j0, HALF)), c[t][:, j0 : j0 + HALF], SUB
-                )
-                dist[j0, t] = keep.tile([P, HALF], F32, name="dist%d_%d" % (j0, t), align_bytes=64)
-                nc.scalar.activation(dist[j0, t][:], diff[:], ABS)
-
-        cand_words, cand_scales = pick("x_cand", cand_list)
-        cand_codes = deal_columns("cand_codes", cand_words, U32)
-        cand_scale = deal_columns("cand_scale", cand_scales, U8)
+        dist = []
+        for t in range(PACK):
+            diff = keep.tile([P, S], F32, name="diff%d" % t, align_bytes=64)
+            nc.vector.tensor_tensor(diff[:], tracks[t][:].indirect(col_list[:]), c[t], SUB)
+            dist.append(keep.tile([P, S], F32, name="dist%d" % t, align_bytes=64))
+            nc.scalar.activation(dist[t][:], diff[:], ABS)
 
         out_codes = keep.tile([P, S], U32, name="out_codes", align_bytes=64)
         out_scales = keep.tile([P, S], U8, name="out_scales", align_bytes=64)
         out_rows = out_0.rearrange("(p t) j -> p t j", t=PACK)
         out_words = out_1[0].rearrange("p n t -> p (n t)").bitcast(I32)
 
-        for j0, n in CHUNKS:
+        def fetch_sum(dst, entries, t, j0, n):
+            nc.vector.tensor_tensor(dst, y[t][:].indirect(entries_of(entries, j0, n)), dist[t][:, j0 : j0 + n], ADD)
+
+        def lower_pair(j0, n):
+            first = keep.tile([P, PACK, n], F32, name="first%d" % j0, align_bytes=64)
+            second = keep.tile([P, PACK, n], F32, name="second%d" % j0, align_bytes=64)
+            for t in range(PACK):
+                fetch_sum(first[:, t, :], di_list, t, j0, n)
+            for t in range(PACK):
+                fetch_sum(second[:, t, :], dj_list, t, j0, n)
+            low = keep.tile([P, PACK, n], F32, name="low%d" % j0, align_bytes=64)
+            nc.vector.tensor_tensor(low[:], first[:], second[:], MIN)
+            return low
+
+        def cells(low, l0, j0, n, by_plane):
+            third = keep.tile([P, PACK, n], F32, name="third%d" % j0, align_bytes=64)
+            cell = keep.tile([P, PACK, n], F32, name="cell%d" % j0, align_bytes=64)
             z_bf = keep.tile([P, n, PACK], BF16, name="z_bf%d" % j0, align_bytes=64)
             for t in range(PACK):
-                h0 = j0 // HALF * HALF
-                u = dist[h0, t][:, j0 - h0 : j0 - h0 + n]
-                sums = []
-                for name, entries in (("a", di_list), ("b", dj_list), ("c", dk_list)):
-                    total = keep.tile([P, n], F32, name="%s%d_%d" % (name, j0, t), align_bytes=64)
-                    nc.vector.tensor_tensor(total[:], y[t][:].indirect(entries_of(entries, j0, n)), u, ADD)
-                    sums.append(total)
-                low = keep.tile([P, n], F32, name="low%d_%d" % (j0, t), align_bytes=64)
-                nc.vector.tensor_tensor(low[:], sums[0][:], sums[1][:], MIN)
-                cell = keep.tile([P, n], F32, name="cell%d_%d" % (j0, t), align_bytes=64)
-                nc.vector.tensor_tensor(cell[:], low[:], sums[2][:], MIN)
-                nc.scalar.activation(z_bf[:, :, t], cell[:], COPY, scale=gains[:, t : t + 1])
+                fetch_sum(third[:, t, :], dk_list, t, j0, n)
+                if by_plane:
+                    nc.vector.tensor_tensor(cell[:, t, :], low[:, t, l0 : l0 + n], third[:, t, :], MIN)
+            if not by_plane:
+                nc.vector.tensor_tensor(cell[:], low[:, :, l0 : l0 + n], third[:], MIN)
+            for t in range(PACK):
+                nc.scalar.activation(z_bf[:, :, t], cell[:, t, :], COPY, scale=gains[:, t : t + 1])
+            return z_bf
+
+        def score_columns(z_bf, j0, n, last):
             z_codes = keep.tile([P, n], U32, name="z_codes%d" % j0, align_bytes=64)
             z_scales = keep.tile([P, n], U8, name="z_scales%d" % j0, align_bytes=64)
             nc.vector.quantize_mx(
@@ -187,7 +206,10 @@ def tile_picked_dtwcell_none_po_kernel(
                         stop=True,
                     )
                 out_bf = keep.tile([P, BLOCK, PACK], BF16, name="out_bf%d" % cols.start, align_bytes=64)
-                nc.scalar.activation(out_bf[:], score[:].rearrange("p t j -> p j t"), COPY, scale=OUT_SCALE)
+                if last:
+                    nc.vector.tensor_scalar_mul(out_bf[:], score[:].rearrange("p t j -> p j t"), OUT_SCALE)
+                else:
+                    nc.scalar.activation(out_bf[:], score[:].rearrange("p t j -> p j t"), COPY, scale=OUT_SCALE)
                 out_f32 = keep.tile([P, PACK, BLOCK], F32, name="out_f32_%d" % cols.start, align_bytes=64)
                 nc.scalar.activation(out_f32[:], score[:], COPY, scale=OUT_SCALE)
                 nc.vector.quantize_mx(
@@ -197,6 +219,12 @@ def tile_picked_dtwcell_none_po_kernel(
                 )
                 nc.sync.dma_start(out_rows[:, :, cols], out_f32[:])
                 nc.sync.dma_start(out_words[:, cols], out_codes[:, cols].bitcast(I32))
+
+        low = lower_pair(0, HALF)
+        score_columns(cells(low, 0, 0, HALF, False), 0, HALF, False)
+        low = lower_pair(HALF, HALF)
+        score_columns(cells(low, 0, HALF, BLOCK, False), HALF, BLOCK, False)
+        score_columns(cells(low, BLOCK, HALF + BLOCK, BLOCK, True), HALF + BLOCK, BLOCK, True)
 
         for q in range(4):
             nc.sync.dma_start(

@@ -3,7 +3,7 @@ from contextlib import ExitStack
 import concourse.mybir as mybir
 
 K, T, S, H, C = 512, 2048, 512, 512, 512
-FLOPS = 2 * K * H * S * 3 + 2 * H * C * S
+FLOPS = 3 * 2 * K * H * S + 2 * H * C * S
 
 F32 = mybir.dt.float32
 BF16 = mybir.dt.bfloat16
@@ -21,10 +21,13 @@ ABS = mybir.ActivationFunctionType.Abs
 
 P = 128
 PACK = 4
+QUADRANTS = 4
+QUADRANT = P // QUADRANTS
+SCALE_ROWS = 4
 LIST_ROWS = 16
-HALF = 256
+HALF = S // 2
 BLOCK = 128
-CHUNKS = ()
+BANKS = 4
 OUT_SCALE = 0.0625
 
 
@@ -44,30 +47,31 @@ def tile_picked_dtwcell_none_po_kernel(
             nc.sync.dma_start(tile[:], src)
             return tile
 
-        def load_words(name, src):
+        def load_fp4_words(name, src):
             tile = keep.tile([P, 2 * H], U8, name=name, align_bytes=64)
             nc.sync.dma_start(tile[:].bitcast(I32), src[0].bitcast(I32))
             return tile
 
         def load_scales(name, src, width):
             tile = keep.tile([P, width], U8, name=name, align_bytes=64)
-            for q in range(4):
-                rows = src[0, 4 * q : 4 * q + 4, :].bitcast(I32)
+            for q in range(QUADRANTS):
+                rows = src[0, SCALE_ROWS * q : SCALE_ROWS * (q + 1), :].bitcast(I32)
                 nc.sync.dma_start(
-                    tile[32 * q : 32 * q + 32, :].bitcast(I32), rows.unsqueeze(0).broadcast_to([8, 4, width // 4])
+                    tile[QUADRANT * q : QUADRANT * (q + 1), :].bitcast(I32),
+                    rows.unsqueeze(0).broadcast_to([QUADRANT // SCALE_ROWS, SCALE_ROWS, width // 4]),
                 )
             return tile
 
         thr_list = load_list("thr_list", thr)
         x_scale_table = load_scales("x_scale_table", x_scales, T)
-        w3_raw = load_words("w3_raw", w3_words)
+        w3_raw = load_fp4_words("w3_raw", w3_words)
         two_list = load_list("two_list", two)
         offs_list = load_list("offs_list", offs)
         x_table = keep.tile([P, T], I32, name="x_table", align_bytes=64)
         nc.sync.dma_start(x_table[:], x_words[0].rearrange("p n t -> p (n t)").bitcast(I32))
-        w2_raw = load_words("w2_raw", w2_words)
+        w2_raw = load_fp4_words("w2_raw", w2_words)
         w3_scale_raw = load_scales("w3_scale_raw", w3_scales, H)
-        w1_raw = load_words("w1_raw", w1_words)
+        w1_raw = load_fp4_words("w1_raw", w1_words)
         cand_list = load_list("cand_list", cand)
         w2_scale_raw = load_scales("w2_scale_raw", w2_scales, H)
         w1_scale_raw = load_scales("w1_scale_raw", w1_scales, H)
@@ -78,9 +82,9 @@ def tile_picked_dtwcell_none_po_kernel(
         gains = keep.tile([P, PACK], F32, name="gains")
         nc.sync.dma_start(gains[:], gs.rearrange("(p t) o -> p (t o)", t=PACK))
 
-        def deal_fp4_words(engine, name, raw):
+        def deal_fp4_words(name, raw):
             dealt = keep.tile([P, 2 * H], U8, name=name, align_bytes=64)
-            engine.tensor_copy(
+            nc.gpsimd.tensor_copy(
                 dealt[:].rearrange("p (t m b) -> p t m b", t=PACK, b=2),
                 raw[:].rearrange("p (m t b) -> p t m b", t=PACK, b=2),
             )
@@ -106,7 +110,7 @@ def tile_picked_dtwcell_none_po_kernel(
 
         def project(planes, w_codes, w_scales, words, scales):
             for t in range(PACK):
-                acc = psum.tile([P, S], F32, name="acc", tag="acc", bufs=6)
+                acc = psum.tile([P, S], F32, name="acc", tag="acc", bufs=BANKS)
                 nc.tensor.matmul_mx(
                     out=acc[:],
                     lhsT=w_codes[:, 2 * P * t : 2 * P * (t + 1)].bitcast(FP4X4),
@@ -120,113 +124,114 @@ def tile_picked_dtwcell_none_po_kernel(
 
         tracks = [keep.tile([P, 2 * S], F32, name="track%d" % t, align_bytes=64) for t in range(PACK)]
         rf = [tracks[t][:, 0:S] for t in range(PACK)]
-        c = [tracks[(t + 1) % PACK][:, S : 2 * S] for t in range(PACK)]
-        y = [keep.tile([P, S], F32, name="y%d" % t, align_bytes=64) for t in range(PACK)]
+        c = [tracks[(t - 1) % PACK][:, S : 2 * S] for t in range(PACK)]
+        costs = [keep.tile([P, 2 * S], F32, name="cost%d" % t, align_bytes=64) for t in range(PACK)]
+        y = [costs[t][:, 0:S] for t in range(PACK)]
+        diff = [costs[t][:, S : 2 * S] for t in range(PACK)]
 
         thr_scales = pick_scales("thr_scales", thr_list)
         two_scales = pick_scales("two_scales", two_list)
         idx_scales = pick_scales("idx_scales", offs_list)
-        w3_codes = deal_fp4_words(nc.gpsimd, "w3_codes", w3_raw)
-        w2_codes = deal_fp4_words(nc.gpsimd, "w2_codes", w2_raw)
+        w3_codes = deal_fp4_words("w3_codes", w3_raw)
+        w2_codes = deal_fp4_words("w2_codes", w2_raw)
         w3_scale = deal_columns(nc.gpsimd, "w3_scale", w3_scale_raw, U8)
         w2_scale = deal_columns(nc.gpsimd, "w2_scale", w2_scale_raw, U8)
-        w1_codes = deal_fp4_words(nc.gpsimd, "w1_codes", w1_raw)
+        w1_codes = deal_fp4_words("w1_codes", w1_raw)
         w1_scale = deal_columns(nc.gpsimd, "w1_scale", w1_scale_raw, U8)
         thr_words = pick_words("thr_words", thr_list)
         project(rf, w3_codes, w3_scale, thr_words, thr_scales)
         two_words = pick_words("two_words", two_list)
         project(c, w2_codes, w2_scale, two_words, two_scales)
         idx_words = pick_words("idx_words", offs_list)
-        project([plane[:] for plane in y], w1_codes, w1_scale, idx_words, idx_scales)
+        project(y, w1_codes, w1_scale, idx_words, idx_scales)
         cand_words = pick_words("cand_words", cand_list)
         cand_scales = pick_scales("cand_scales", cand_list)
         cand_codes = deal_columns(nc.vector, "cand_codes", cand_words, U32)
         cand_scale = deal_columns(nc.vector, "cand_scale", cand_scales, U8)
 
-        def entries_of(tile, j0, n):
-            return tile[:, j0 // LIST_ROWS : (j0 + n) // LIST_ROWS]
-
         dist = []
         for t in range(PACK):
-            diff = keep.tile([P, S], F32, name="diff%d" % t, align_bytes=64)
-            nc.vector.tensor_tensor(diff[:], tracks[t][:].indirect(col_list[:]), c[t], SUB)
+            nc.vector.tensor_tensor(diff[t], tracks[t][:].indirect(col_list[:]), c[t], SUB)
             dist.append(keep.tile([P, S], F32, name="dist%d" % t, align_bytes=64))
-            nc.scalar.activation(dist[t][:], diff[:], ABS)
+            nc.scalar.activation(dist[t][:], diff[t], ABS)
 
+        z_bf = keep.tile([P, S, PACK], BF16, name="z_bf", align_bytes=64)
+        z_codes = keep.tile([P, S], U32, name="z_codes", align_bytes=64)
+        z_scales = keep.tile([P, S], U8, name="z_scales", align_bytes=64)
+
+        def fetch_sum(name, entries, t, cols):
+            total = keep.tile([P, cols.stop - cols.start], F32, name=name, align_bytes=64)
+            offsets = entries[:, cols.start // LIST_ROWS : cols.stop // LIST_ROWS]
+            nc.vector.tensor_tensor(total[:], costs[t][:].indirect(offsets), dist[t][:, cols], ADD)
+            return total
+
+        def score_block(cols):
+            nc.vector.quantize_mx(
+                out=z_codes[:, cols].bitcast(FP8X4),
+                scales=z_scales[:, cols],
+                in_=z_bf[:, cols, :].rearrange("p j t -> p (j t)"),
+            )
+            score = psum.tile([P, PACK, BLOCK], F32, name="score", tag="score", bufs=BANKS)
+            for t in range(PACK):
+                nc.tensor.matmul_mx(
+                    out=score[:, t, :],
+                    lhsT=cand_codes[:, P * t : P * (t + 1)].bitcast(FP8X4),
+                    lhsT_scale=cand_scale[:, P * t : P * (t + 1)],
+                    rhs=z_codes[:, cols].bitcast(FP8X4),
+                    rhs_scale=z_scales[:, cols],
+                    start=True,
+                    stop=True,
+                )
+            return score
+
+        scores = []
+        for t in range(PACK):
+            last_plane = t == PACK - 1
+            first = fetch_sum("first%d" % t, di_list, t, slice(0, S))
+            second = fetch_sum("second%d" % t, dj_list, t, slice(0, S))
+            low = keep.tile([P, S], F32, name="low%d" % t, align_bytes=64)
+            cell = keep.tile([P, S], F32, name="cell%d" % t, align_bytes=64)
+            min_width = HALF if last_plane else S
+            weigh_width = BLOCK if last_plane else S
+            for j0 in range(0, S, min_width):
+                cols = slice(j0, j0 + min_width)
+                nc.vector.tensor_tensor(low[:, cols], first[:, cols], second[:, cols], MIN)
+                third = fetch_sum("third%d_%d" % (t, j0), dk_list, t, cols)
+                nc.vector.tensor_tensor(cell[:, cols], low[:, cols], third[:], MIN)
+                for b0 in range(j0, j0 + min_width, weigh_width):
+                    block = slice(b0, b0 + weigh_width)
+                    nc.scalar.activation(z_bf[:, block, t], cell[:, block], COPY, scale=gains[:, t : t + 1])
+                    if last_plane:
+                        scores.append(score_block(block))
+
+        out_bf = keep.tile([P, S, PACK], BF16, name="out_bf", align_bytes=64)
         out_codes = keep.tile([P, S], U32, name="out_codes", align_bytes=64)
         out_scales = keep.tile([P, S], U8, name="out_scales", align_bytes=64)
         out_rows = out_0.rearrange("(p t) j -> p t j", t=PACK)
         out_words = out_1[0].rearrange("p n t -> p (n t)").bitcast(I32)
-
-        def fetch_sum(dst, entries, t, j0, n):
-            nc.vector.tensor_tensor(dst, y[t][:].indirect(entries_of(entries, j0, n)), dist[t][:, j0 : j0 + n], ADD)
-
-        def lower_pair(j0, n):
-            first = keep.tile([P, PACK, n], F32, name="first%d" % j0, align_bytes=64)
-            second = keep.tile([P, PACK, n], F32, name="second%d" % j0, align_bytes=64)
-            for t in range(PACK):
-                fetch_sum(first[:, t, :], di_list, t, j0, n)
-            for t in range(PACK):
-                fetch_sum(second[:, t, :], dj_list, t, j0, n)
-            low = keep.tile([P, PACK, n], F32, name="low%d" % j0, align_bytes=64)
-            nc.vector.tensor_tensor(low[:], first[:], second[:], MIN)
-            return low
-
-        def cells(low, l0, j0, n, by_plane):
-            third = keep.tile([P, PACK, n], F32, name="third%d" % j0, align_bytes=64)
-            cell = keep.tile([P, PACK, n], F32, name="cell%d" % j0, align_bytes=64)
-            z_bf = keep.tile([P, n, PACK], BF16, name="z_bf%d" % j0, align_bytes=64)
-            for t in range(PACK):
-                fetch_sum(third[:, t, :], dk_list, t, j0, n)
-                if by_plane:
-                    nc.vector.tensor_tensor(cell[:, t, :], low[:, t, l0 : l0 + n], third[:, t, :], MIN)
-            if not by_plane:
-                nc.vector.tensor_tensor(cell[:], low[:, :, l0 : l0 + n], third[:], MIN)
-            for t in range(PACK):
-                nc.scalar.activation(z_bf[:, :, t], cell[:, t, :], COPY, scale=gains[:, t : t + 1])
-            return z_bf
-
-        def score_columns(z_bf, j0, n, last):
-            z_codes = keep.tile([P, n], U32, name="z_codes%d" % j0, align_bytes=64)
-            z_scales = keep.tile([P, n], U8, name="z_scales%d" % j0, align_bytes=64)
-            nc.vector.quantize_mx(
-                out=z_codes[:].bitcast(FP8X4), scales=z_scales[:], in_=z_bf[:].rearrange("p j t -> p (j t)")
-            )
-            for b0 in range(0, n, BLOCK):
-                cols = slice(j0 + b0, j0 + b0 + BLOCK)
-                score = psum.tile([P, PACK, BLOCK], F32, name="score", tag="score", bufs=2)
-                for t in range(PACK):
-                    nc.tensor.matmul_mx(
-                        out=score[:, t, :],
-                        lhsT=cand_codes[:, P * t : P * (t + 1)].bitcast(FP8X4),
-                        lhsT_scale=cand_scale[:, P * t : P * (t + 1)],
-                        rhs=z_codes[:, b0 : b0 + BLOCK].bitcast(FP8X4),
-                        rhs_scale=z_scales[:, b0 : b0 + BLOCK],
-                        start=True,
-                        stop=True,
-                    )
-                out_bf = keep.tile([P, BLOCK, PACK], BF16, name="out_bf%d" % cols.start, align_bytes=64)
-                if last:
-                    nc.vector.tensor_scalar_mul(out_bf[:], score[:].rearrange("p t j -> p j t"), OUT_SCALE)
-                else:
-                    nc.scalar.activation(out_bf[:], score[:].rearrange("p t j -> p j t"), COPY, scale=OUT_SCALE)
-                out_f32 = keep.tile([P, PACK, BLOCK], F32, name="out_f32_%d" % cols.start, align_bytes=64)
+        for b, score in enumerate(scores):
+            block = slice(b * BLOCK, (b + 1) * BLOCK)
+            out_f32 = keep.tile([P, PACK, BLOCK], F32, name="out_f32_%d" % b, align_bytes=64)
+            if b == len(scores) - 1:
+                nc.vector.tensor_scalar_mul(out_bf[:, block, :], score[:].rearrange("p t j -> p j t"), OUT_SCALE)
                 nc.scalar.activation(out_f32[:], score[:], COPY, scale=OUT_SCALE)
+                nc.scalar.dma_start(out_rows[:, :, block], out_f32[:])
+            else:
+                nc.scalar.activation(out_f32[:], score[:], COPY, scale=OUT_SCALE)
+                nc.sync.dma_start(out_rows[:, :, block], out_f32[:])
+                nc.vector.tensor_copy(out_bf[:, block, :], out_f32[:].rearrange("p t j -> p j t"))
+            if block.stop % HALF == 0:
+                cols = slice(block.stop - HALF, block.stop)
                 nc.vector.quantize_mx(
                     out=out_codes[:, cols].bitcast(FP8X4),
                     scales=out_scales[:, cols],
-                    in_=out_bf[:].rearrange("p j t -> p (j t)"),
+                    in_=out_bf[:, cols, :].rearrange("p j t -> p (j t)"),
                 )
-                nc.sync.dma_start(out_rows[:, :, cols], out_f32[:])
                 nc.sync.dma_start(out_words[:, cols], out_codes[:, cols].bitcast(I32))
 
-        low = lower_pair(0, HALF)
-        score_columns(cells(low, 0, 0, HALF, False), 0, HALF, False)
-        low = lower_pair(HALF, HALF)
-        score_columns(cells(low, 0, HALF, BLOCK, False), HALF, BLOCK, False)
-        score_columns(cells(low, BLOCK, HALF + BLOCK, BLOCK, True), HALF + BLOCK, BLOCK, True)
-
-        for q in range(4):
-            nc.sync.dma_start(
-                out_2[0, 4 * q : 4 * q + 4, :].bitcast(I32), out_scales[32 * q : 32 * q + 4, :].bitcast(I32)
+        for q in range(QUADRANTS):
+            queue = nc.sync if q < QUADRANTS // 2 else nc.scalar
+            queue.dma_start(
+                out_2[0, SCALE_ROWS * q : SCALE_ROWS * (q + 1), :].bitcast(I32),
+                out_scales[QUADRANT * q : QUADRANT * q + SCALE_ROWS, :].bitcast(I32),
             )

from contextlib import ExitStack

import concourse.mybir as mybir

K, T, S, H, C = 512, 2048, 512, 512, 512
FLOPS = 3 * 2 * K * H * S + 2 * H * C * S

F32 = mybir.dt.float32
BF16 = mybir.dt.bfloat16
I32 = mybir.dt.int32
U32 = mybir.dt.uint32
U16 = mybir.dt.uint16
U8 = mybir.dt.uint8
FP8X4 = mybir.dt.float8_e4m3fn_x4
FP4X4 = mybir.dt.float4_e2m1fn_x4
ADD = mybir.AluOpType.add
SUB = mybir.AluOpType.subtract
MIN = mybir.AluOpType.min
COPY = mybir.ActivationFunctionType.Copy
ABS = mybir.ActivationFunctionType.Abs

P = 128
PACK = 4
QUADRANTS = 4
QUADRANT = P // QUADRANTS
SCALE_ROWS = 4
LIST_ROWS = 16
HALF = S // 2
BLOCK = 128
BANKS = 4
OUT_SCALE = 0.0625


def tile_picked_dtwcell_none_po_kernel(
    tc, x_words, x_scales, w1_words, w1_scales, w2_words, w2_scales, w3_words, w3_scales,
    gs, offs, two, thr, di, dj, dk, col, cand, out_0, out_1, out_2,
):
    nc = tc.nc

    with ExitStack() as ctx:
        lists = ctx.enter_context(tc.tile_pool(name="lists", bufs=1))
        keep = ctx.enter_context(tc.tile_pool(name="keep", bufs=1))
        psum = ctx.enter_context(tc.psum_pool(name="psum", bufs=1))

        def load_list(name, src):
            tile = lists.tile([P, S // LIST_ROWS], U16, name=name)
            nc.sync.dma_start(tile[:], src)
            return tile

        def load_fp4_words(name, src):
            tile = keep.tile([P, 2 * H], U8, name=name, align_bytes=64)
            nc.sync.dma_start(tile[:].bitcast(I32), src[0].bitcast(I32))
            return tile

        def load_scales(name, src, width):
            tile = keep.tile([P, width], U8, name=name, align_bytes=64)
            for q in range(QUADRANTS):
                rows = src[0, SCALE_ROWS * q : SCALE_ROWS * (q + 1), :].bitcast(I32)
                nc.sync.dma_start(
                    tile[QUADRANT * q : QUADRANT * (q + 1), :].bitcast(I32),
                    rows.unsqueeze(0).broadcast_to([QUADRANT // SCALE_ROWS, SCALE_ROWS, width // 4]),
                )
            return tile

        thr_list = load_list("thr_list", thr)
        x_scale_table = load_scales("x_scale_table", x_scales, T)
        w3_raw = load_fp4_words("w3_raw", w3_words)
        two_list = load_list("two_list", two)
        offs_list = load_list("offs_list", offs)
        x_table = keep.tile([P, T], I32, name="x_table", align_bytes=64)
        nc.sync.dma_start(x_table[:], x_words[0].rearrange("p n t -> p (n t)").bitcast(I32))
        w2_raw = load_fp4_words("w2_raw", w2_words)
        w3_scale_raw = load_scales("w3_scale_raw", w3_scales, H)
        w1_raw = load_fp4_words("w1_raw", w1_words)
        cand_list = load_list("cand_list", cand)
        w2_scale_raw = load_scales("w2_scale_raw", w2_scales, H)
        w1_scale_raw = load_scales("w1_scale_raw", w1_scales, H)
        col_list = load_list("col_list", col)
        di_list = load_list("di_list", di)
        dj_list = load_list("dj_list", dj)
        dk_list = load_list("dk_list", dk)
        gains = keep.tile([P, PACK], F32, name="gains")
        nc.sync.dma_start(gains[:], gs.rearrange("(p t) o -> p (t o)", t=PACK))

        def deal_fp4_words(name, raw):
            dealt = keep.tile([P, 2 * H], U8, name=name, align_bytes=64)
            nc.gpsimd.tensor_copy(
                dealt[:].rearrange("p (t m b) -> p t m b", t=PACK, b=2),
                raw[:].rearrange("p (m t b) -> p t m b", t=PACK, b=2),
            )
            return dealt

        def deal_columns(engine, name, raw, dtype):
            dealt = keep.tile([P, H], dtype, name=name, align_bytes=64)
            engine.tensor_copy(
                dealt[:].rearrange("p (t m) -> p t m", t=PACK),
                raw[:].rearrange("p (m t) -> p t m", t=PACK),
            )
            return dealt

        def pick_words(name, entries):
            words = keep.tile([P, S], U32, name=name, align_bytes=64)
            nc.vector.tensor_copy(words[:], x_table[:].bitcast(U32).indirect(entries[:]))
            return words

        def pick_scales(name, entries):
            scales = keep.tile([P, S], U8, name=name, align_bytes=64)
            nc.vector.tensor_copy(scales[:], x_scale_table[:].indirect(entries[:]))
            return scales

        def project(planes, w_codes, w_scales, words, scales):
            for t in range(PACK):
                acc = psum.tile([P, S], F32, name="acc", tag="acc", bufs=BANKS)
                nc.tensor.matmul_mx(
                    out=acc[:],
                    lhsT=w_codes[:, 2 * P * t : 2 * P * (t + 1)].bitcast(FP4X4),
                    lhsT_scale=w_scales[:, P * t : P * (t + 1)],
                    rhs=words[:].bitcast(FP8X4),
                    rhs_scale=scales[:],
                    start=True,
                    stop=True,
                )
                nc.scalar.copy(planes[t], acc[:])

        tracks = [keep.tile([P, 2 * S], F32, name="track%d" % t, align_bytes=64) for t in range(PACK)]
        rf = [tracks[t][:, 0:S] for t in range(PACK)]
        c = [tracks[(t - 1) % PACK][:, S : 2 * S] for t in range(PACK)]
        costs = [keep.tile([P, 2 * S], F32, name="cost%d" % t, align_bytes=64) for t in range(PACK)]
        y = [costs[t][:, 0:S] for t in range(PACK)]
        diff = [costs[t][:, S : 2 * S] for t in range(PACK)]

        thr_scales = pick_scales("thr_scales", thr_list)
        two_scales = pick_scales("two_scales", two_list)
        idx_scales = pick_scales("idx_scales", offs_list)
        w3_codes = deal_fp4_words("w3_codes", w3_raw)
        w2_codes = deal_fp4_words("w2_codes", w2_raw)
        w3_scale = deal_columns(nc.gpsimd, "w3_scale", w3_scale_raw, U8)
        w2_scale = deal_columns(nc.gpsimd, "w2_scale", w2_scale_raw, U8)
        w1_codes = deal_fp4_words("w1_codes", w1_raw)
        w1_scale = deal_columns(nc.gpsimd, "w1_scale", w1_scale_raw, U8)
        thr_words = pick_words("thr_words", thr_list)
        project(rf, w3_codes, w3_scale, thr_words, thr_scales)
        two_words = pick_words("two_words", two_list)
        project(c, w2_codes, w2_scale, two_words, two_scales)
        idx_words = pick_words("idx_words", offs_list)
        project(y, w1_codes, w1_scale, idx_words, idx_scales)
        cand_words = pick_words("cand_words", cand_list)
        cand_scales = pick_scales("cand_scales", cand_list)
        cand_codes = deal_columns(nc.vector, "cand_codes", cand_words, U32)
        cand_scale = deal_columns(nc.vector, "cand_scale", cand_scales, U8)

        dist = []
        for t in range(PACK):
            nc.vector.tensor_tensor(diff[t], tracks[t][:].indirect(col_list[:]), c[t], SUB)
            dist.append(keep.tile([P, S], F32, name="dist%d" % t, align_bytes=64))
            nc.scalar.activation(dist[t][:], diff[t], ABS)

        z_bf = keep.tile([P, S, PACK], BF16, name="z_bf", align_bytes=64)
        z_codes = keep.tile([P, S], U32, name="z_codes", align_bytes=64)
        z_scales = keep.tile([P, S], U8, name="z_scales", align_bytes=64)

        def fetch_sum(name, entries, t, cols):
            total = keep.tile([P, cols.stop - cols.start], F32, name=name, align_bytes=64)
            offsets = entries[:, cols.start // LIST_ROWS : cols.stop // LIST_ROWS]
            nc.vector.tensor_tensor(total[:], costs[t][:].indirect(offsets), dist[t][:, cols], ADD)
            return total

        def score_block(cols):
            nc.vector.quantize_mx(
                out=z_codes[:, cols].bitcast(FP8X4),
                scales=z_scales[:, cols],
                in_=z_bf[:, cols, :].rearrange("p j t -> p (j t)"),
            )
            score = psum.tile([P, PACK, BLOCK], F32, name="score", tag="score", bufs=BANKS)
            for t in range(PACK):
                nc.tensor.matmul_mx(
                    out=score[:, t, :],
                    lhsT=cand_codes[:, P * t : P * (t + 1)].bitcast(FP8X4),
                    lhsT_scale=cand_scale[:, P * t : P * (t + 1)],
                    rhs=z_codes[:, cols].bitcast(FP8X4),
                    rhs_scale=z_scales[:, cols],
                    start=True,
                    stop=True,
                )
            return score

        scores = []
        for t in range(PACK):
            last_plane = t == PACK - 1
            first = fetch_sum("first%d" % t, di_list, t, slice(0, S))
            second = fetch_sum("second%d" % t, dj_list, t, slice(0, S))
            low = keep.tile([P, S], F32, name="low%d" % t, align_bytes=64)
            cell = keep.tile([P, S], F32, name="cell%d" % t, align_bytes=64)
            min_width = HALF if last_plane else S
            weigh_width = BLOCK if last_plane else S
            for j0 in range(0, S, min_width):
                cols = slice(j0, j0 + min_width)
                nc.vector.tensor_tensor(low[:, cols], first[:, cols], second[:, cols], MIN)
                third = fetch_sum("third%d_%d" % (t, j0), dk_list, t, cols)
                nc.vector.tensor_tensor(cell[:, cols], low[:, cols], third[:], MIN)
                for b0 in range(j0, j0 + min_width, weigh_width):
                    block = slice(b0, b0 + weigh_width)
                    nc.scalar.activation(z_bf[:, block, t], cell[:, block], COPY, scale=gains[:, t : t + 1])
                    if last_plane:
                        scores.append(score_block(block))

        out_bf = keep.tile([P, S, PACK], BF16, name="out_bf", align_bytes=64)
        out_codes = keep.tile([P, S], U32, name="out_codes", align_bytes=64)
        out_scales = keep.tile([P, S], U8, name="out_scales", align_bytes=64)
        out_rows = out_0.rearrange("(p t) j -> p t j", t=PACK)
        out_words = out_1[0].rearrange("p n t -> p (n t)").bitcast(I32)
        for b, score in enumerate(scores):
            block = slice(b * BLOCK, (b + 1) * BLOCK)
            out_f32 = keep.tile([P, PACK, BLOCK], F32, name="out_f32_%d" % b, align_bytes=64)
            if b == len(scores) - 1:
                nc.vector.tensor_scalar_mul(out_bf[:, block, :], score[:].rearrange("p t j -> p j t"), OUT_SCALE)
                nc.scalar.activation(out_f32[:], score[:], COPY, scale=OUT_SCALE)
                nc.scalar.dma_start(out_rows[:, :, block], out_f32[:])
            else:
                nc.scalar.activation(out_f32[:], score[:], COPY, scale=OUT_SCALE)
                nc.sync.dma_start(out_rows[:, :, block], out_f32[:])
                nc.vector.tensor_copy(out_bf[:, block, :], out_f32[:].rearrange("p t j -> p j t"))
            if block.stop % HALF == 0:
                cols = slice(block.stop - HALF, block.stop)
                nc.vector.quantize_mx(
                    out=out_codes[:, cols].bitcast(FP8X4),
                    scales=out_scales[:, cols],
                    in_=out_bf[:, cols, :].rearrange("p j t -> p (j t)"),
                )
                nc.sync.dma_start(out_words[:, cols], out_codes[:, cols].bitcast(I32))

        for q in range(QUADRANTS):
            queue = nc.sync if q < QUADRANTS // 2 else nc.scalar
            queue.dma_start(
                out_2[0, SCALE_ROWS * q : SCALE_ROWS * (q + 1), :].bitcast(I32),
                out_scales[QUADRANT * q : QUADRANT * q + SCALE_ROWS, :].bitcast(I32),
            )
